import numpy as np
import ml_dtypes


def mxq(x, axis, fmt="e4m3"):
    dtype, down = {"e4m3": (ml_dtypes.float8_e4m3fn, 7), "e5m2": (ml_dtypes.float8_e5m2, 14)}[fmt]
    v = np.moveaxis(np.asarray(x, np.float32).astype(ml_dtypes.bfloat16).astype(np.float64), axis, -1)
    blocks = v.reshape(v.shape[:-1] + (-1, 32))
    amax = np.abs(blocks).max(-1, keepdims=True)
    byte = np.maximum(np.where(amax > 0, np.frexp(amax)[1] - 1 + 127, 0) - down, 1)
    scale = np.exp2(byte - 127.0)
    codes = (blocks / scale).astype(np.float32).astype(dtype).astype(np.float64)
    return np.moveaxis((codes * scale).reshape(v.shape), -1, axis)


WIDE = False


def mx_kscale(k):
    if not WIDE:
        return np.ones(k)
    levels = np.array([24, -24, 12, -12, 0])
    if k % 512:
        return np.exp2(np.random.permutation(np.resize(levels, k // 32))).repeat(32)
    a = np.empty((k // 512, 16))
    for p in range(k // 512):
        a[p, :8] = np.random.permutation(np.resize(levels, 8))
        for g in range(8):
            far = levels[np.abs(levels - a[p, g]) >= 10]
            a[p, g + 8] = far[np.random.randint(len(far))]
    return np.exp2(a.ravel()).repeat(32)


def f64(x):
    return np.asarray(x).astype(np.float64)


def striped8(idx):
    return np.concatenate([v.reshape(-1, 16).T for v in idx]).astype(np.uint16)


def unstriped8(offs):
    return np.stack([offs[16 * g:16 * g + 16].T.reshape(-1) for g in range(8)]).astype(np.int64)


E2M1 = np.array([0.0, 0.5, 1.0, 1.5, 2.0, 3.0, 4.0, 6.0, -0.0, -0.5, -1.0, -1.5, -2.0, -3.0, -4.0, -6.0])


def pack_weight(w, fmt):
    k, n = w.shape
    w = f64(np.asarray(w, np.float32).astype(ml_dtypes.bfloat16)).reshape(k // 32, 32, n)
    amax = np.abs(w).max(1)
    if fmt == "e4m3":
        byte = np.frexp(amax)[1] - 1 + 127 - 7
    else:
        mant, ex = np.frexp(amax / 6.0)
        byte = np.where(mant > 0.5, ex, ex - 1) + 127
    byte = np.clip(np.where(amax > 0, byte, 1), 1, 254)
    scaled = (w * np.exp2(127.0 - byte)[:, None, :]).reshape(k, n).astype(np.float32)
    by_word = np.ascontiguousarray(scaled.reshape(k // 512, 128, 4, n).transpose(0, 1, 3, 2))
    if fmt == "e4m3":
        words = by_word.astype(ml_dtypes.float8_e4m3fn).view(np.uint8)
    else:
        c = by_word.astype(ml_dtypes.float4_e2m1fn).view(np.uint8) & 0xF
        words = (c[..., 0::2] | (c[..., 1::2] << 4)).reshape(k // 512, 128, 2 * n)
    return np.ascontiguousarray(words), np.ascontiguousarray(byte.astype(np.uint8).reshape(k // 512, 16, n))


def unpack_weight(words, scales, fmt):
    g, _, n = scales.shape
    words = np.ascontiguousarray(words).reshape(g, 128, n, -1)
    if fmt == "e4m3":
        vals = words.view(ml_dtypes.float8_e4m3fn).astype(np.float64)
    else:
        nib = np.empty((g, 128, n, 4), np.uint8)
        nib[..., 0::2] = words & 0xF
        nib[..., 1::2] = words >> 4
        vals = E2M1[nib]
    vals = vals * np.repeat(np.exp2(scales.astype(np.float64) - 127.0), 8, axis=1)[..., None]
    return vals.transpose(0, 1, 3, 2).reshape(g * 512, n)


def planes(y):
    n, m = y.shape
    v = y.astype(np.float32).astype(ml_dtypes.bfloat16).astype(np.float64).reshape(n // 32, 32, m)
    top = np.abs(v).max(1)
    byte = np.clip(np.where(top > 0, np.frexp(top)[1] - 1 + 127 - 7, 1), 1, 254)
    codes = (v * np.exp2(127.0 - byte)[:, None, :]).reshape(n, m).astype(np.float32).astype(ml_dtypes.float8_e4m3fn).view(np.uint8)
    words = codes.reshape(n // 512, 128, 4, m).transpose(0, 1, 3, 2)
    return np.ascontiguousarray(words), np.ascontiguousarray(byte.astype(np.uint8).reshape(n // 512, 16, m))


def silu(f):
    return f / (1.0 + np.exp(-np.maximum(f, -700.0)))


K, L, N, T, J = 512, 512, 512, 2048, 1024


def setup_inputs():
    n = np.random.standard_normal
    s = mx_kscale(K)[:, None]
    s2 = mx_kscale(L)[:, None]
    p_wx = pack_weight(n((L, N)) / np.sqrt(L) / s2, "e4m3")
    return {
        "xT": (n((K, T)) * s).astype(np.float32),
        "wgt": np.repeat(np.random.uniform(0.5, 2.0, (8, J)), 16, axis=0).astype(np.float32),
        "wt": (n((K, N)) / np.sqrt(K) / s).astype(np.float32),
        "c": (n((L, J)) * s2).astype(np.float32),
        "wx_words": p_wx[0],
        "wx_scales": p_wx[1],
        "b": (0.3 * n(N)).astype(np.float32),
        "offs": striped8(np.stack([np.random.permutation(T)[:J] for _ in range(8)])),
    }


def reference(xT, wgt, wt, c, wx_words, wx_scales, b, offs):
    idx = unstriped8(offs)
    rows = np.arange(K)
    xg = f64(wgt)[rows // 4 % 128] * f64(xT)[rows[:, None], idx[rows % 512 // 64]]
    xT_ = mxq(xg, 0, "e4m3")
    wt_ = mxq(f64(wt), 0, "e4m3")
    c_q_ = mxq(f64(c), 0, "e4m3")
    c_r_ = mxq(f64(c) - c_q_, 0, "e4m3")
    wx_ = unpack_weight(wx_words, wx_scales, "e4m3")
    y = wt_.T @ xT_ + wx_.T @ c_q_ + wx_.T @ c_r_
    out_0 = silu(y + f64(b)[:, None])
    return (out_0,) + planes(out_0)

@@ -1,0 +1,247 @@
+from contextlib import ExitStack
+
+import concourse.mybir as mybir
+
+K, L, N, T, J = 512, 512, 512, 2048, 1024
+FLOPS = 2 * N * J * (K + 2 * L) + 2 * L * L * J
+
+F32 = mybir.dt.float32
+BF16 = mybir.dt.bfloat16
+I32 = mybir.dt.int32
+U32 = mybir.dt.uint32
+U16 = mybir.dt.uint16
+U8 = mybir.dt.uint8
+FP8X4 = mybir.dt.float8_e4m3fn_x4
+ALU = mybir.AluOpType
+ACT = mybir.ActivationFunctionType
+
+P = 128
+PACK = 4
+QW = 256
+NQ = J // QW
+HALF = 512
+
+
+def planes_walk(ap):
+    return ap.rearrange("p t (c i) -> p c t i", i=4)
+
+
+def woven_walk(ap):
+    return ap.rearrange("p (c i t) -> p c t i", i=4, t=PACK)
+
+
+def tile_list_siluP_kernel(
+    tc, xT, wgt, wt, c, wx_words, wx_scales, b, offs, out_0, out_1, out_2
+):
+    nc = tc.nc
+    with ExitStack() as ctx:
+        keep = ctx.enter_context(tc.tile_pool(name="keep", bufs=1))
+        psum = ctx.enter_context(tc.psum_pool(name="psum", bufs=1))
+
+        def operand(name, width):
+            codes = keep.tile([P, width], U32, name=name + "_codes", align_bytes=64)
+            scales = keep.tile([P, width], U8, name=name + "_scales", align_bytes=64)
+            return codes, scales
+
+        def quantize(op, cols, woven):
+            nc.vector.quantize_mx(out=op[0][:, cols].bitcast(FP8X4), scales=op[1][:, cols], in_=woven)
+
+        def mx_pass(out, stat, stat_cols, mov, mov_cols, start, stop):
+            nc.tensor.matmul_mx(
+                out=out,
+                lhsT=stat[0][:, stat_cols].bitcast(FP8X4),
+                lhsT_scale=stat[1][:, stat_cols],
+                rhs=mov[0][:, mov_cols].bitcast(FP8X4),
+                rhs_scale=mov[1][:, mov_cols],
+                start=start,
+                stop=stop,
+            )
+
+        c_rows = c.rearrange("(p t) j -> p t j", t=PACK)
+        x_planes = xT.rearrange("(p t) s -> t p s", t=PACK)
+        c_raw = []
+        def load_c(lo, hi):
+            tl = keep.tile([P, PACK, hi - lo], F32, name="c_raw%d" % lo)
+            nc.sync.dma_start(out=tl[:], in_=c_rows[:, :, lo:hi])
+            for q0 in range(lo, hi, QW):
+                c_raw.append(tl[:, :, q0 - lo : q0 - lo + QW])
+        wt_raw = keep.tile([P, PACK, N], F32)
+        wxw_raw = keep.tile([P, N], I32)
+        wxs_raw = keep.tile([P, N], U8)
+        offsets = keep.tile([P, J // 16], U16)
+        wgt_sb = keep.tile([P, J], F32)
+        bias = keep.tile([P, PACK], F32)
+        x_sb = [keep.tile([P, T], F32, name="x_plane%d" % t) for t in range(PACK)]
+        nc.gpsimd.memset(wxs_raw[:].bitcast(I32), 0)
+        load_c(0, 256)
+        load_c(256, 512)
+        for Q in range(4):
+            nc.sync.dma_start(out=wxs_raw[32 * Q : 32 * Q + 4, :].bitcast(I32), in_=wx_scales[0, 4 * Q : 4 * Q + 4, :].bitcast(I32))
+        nc.sync.dma_start(out=wt_raw[:], in_=wt.rearrange("(p j) n -> p j n", j=PACK))
+        load_c(512, 1024)
+        nc.sync.dma_start(out=wxw_raw[:], in_=wx_words[0].rearrange("p n i -> p (n i)").bitcast(I32))
+        nc.sync.dma_start(offsets[:], offs)
+        nc.sync.dma_start(out=wgt_sb[:], in_=wgt)
+        nc.sync.dma_start(out=x_sb[0][:], in_=x_planes[0])
+        nc.sync.dma_start(out=bias[:], in_=b.rearrange("(p t) -> p t", t=PACK))
+        nc.sync.dma_start(out=x_sb[1][:], in_=x_planes[1])
+        nc.sync.dma_start(out=x_sb[2][:], in_=x_planes[2])
+        nc.sync.dma_start(out=x_sb[3][:], in_=x_planes[3])
+
+        ramp = keep.tile([P, P], F32)
+        nc.gpsimd.iota(ramp[:], pattern=[[1, P]], base=0, channel_multiplier=-1, allow_small_or_imprecise_dtypes=True)
+        ident_bf = keep.tile([P, PACK * (P * PACK + 1)], BF16, align_bytes=64)
+        nc.vector.memset(ident_bf[:].bitcast(I32), 0)
+        nc.vector.tensor_scalar(
+            out=ident_bf[:].rearrange("p (t r) -> p t r", t=PACK)[:, :, 0 : P * PACK : PACK],
+            in0=ramp[:].unsqueeze(1).to_broadcast([P, PACK, P]),
+            scalar1=0.0,
+            scalar2=None,
+            op0=ALU.is_equal,
+        )
+        ident = operand("ident", PACK * P)
+        quantize(ident, slice(0, PACK * P), ident_bf[:, 0 : PACK * P * PACK])
+        cq = [operand("cq%d" % q, QW) for q in range(NQ)]
+        cr = [operand("cr%d" % q, QW) for q in range(NQ)]
+        xg = [operand("xg%d" % q, QW) for q in range(NQ)]
+        wtq = operand("wt", N)
+        wxq = operand("wx", N)
+        yq = operand("y", J)
+        allq = slice(0, QW)
+
+        def c_first(q):
+            woven = keep.tile([P, QW * PACK], BF16, name="c_woven%d" % q, align_bytes=64)
+            nc.scalar.copy(out=woven_walk(woven[:]), in_=planes_walk(c_raw[q]))
+            quantize(cq[q], allq, woven[:])
+
+        def c_second(q):
+            woven = keep.tile([P, QW * PACK], BF16, name="r_woven%d" % q, align_bytes=64)
+            for u in range(2):
+                cols = slice(u * P, (u + 1) * P)
+                back = psum.tile([P, PACK, P], F32, name="back%d_%d" % (q, u), tag="bank%d" % (2 * q + u))
+                for t in range(PACK):
+                    mx_pass(back[:, t, :], ident, slice(t * P, (t + 1) * P), cq[q], cols, True, True)
+                nc.vector.tensor_tensor(
+                    out=woven_walk(woven[:, u * P * PACK : (u + 1) * P * PACK]),
+                    in0=planes_walk(c_raw[q][:, :, cols]),
+                    in1=planes_walk(back[:]),
+                    op=ALU.subtract,
+                )
+            quantize(cr[q], allq, woven[:])
+
+        def make_wt():
+            woven = keep.tile([P, N * PACK], BF16, name="wt_woven", align_bytes=64)
+            nc.scalar.copy(
+                out=woven[:].rearrange("p (t m j) -> p m j t", t=PACK, j=PACK),
+                in_=wt_raw[:].rearrange("p j (m t) -> p m j t", t=PACK),
+            )
+            quantize(wtq, slice(0, N), woven[:])
+
+        def make_wx():
+            nc.vector.tensor_copy(
+                out=wxq[0][:].bitcast(I32).rearrange("p (t h m) -> p h t m", t=PACK, m=4),
+                in_=wxw_raw[:].rearrange("p (h m t) -> p h t m", t=PACK, m=4),
+            )
+            nc.vector.tensor_copy(
+                out=wxq[1][:].rearrange("p (t m) -> p t m", t=PACK),
+                in_=wxs_raw[:].rearrange("p (m t) -> p t m", t=PACK),
+            )
+
+        acc = {}
+
+        def tier_passes(q):
+            for u in range(2):
+                acc[q, u] = psum.tile([P, 2, QW], F32, name="acc%d_%d" % (q, u), tag="bank%d" % (2 * q + u))
+                for v in range(2):
+                    t = 2 * u + v
+                    mx_pass(acc[q, u][:, v, :], wxq, slice(t * P, (t + 1) * P), cq[q], allq, v == 0, False)
+                    mx_pass(acc[q, u][:, v, :], wxq, slice(t * P, (t + 1) * P), cr[q], allq, False, False)
+
+        GW = 512
+        picked = [keep.tile([P, PACK, GW], F32, name="picked%d" % h) for h in range(J // GW)]
+
+        def gather(t, h):
+            lists = offsets[:, h * GW // 16 : (h + 1) * GW // 16]
+            nc.vector.tensor_tensor(picked[h][:, t, :], x_sb[t][:].indirect(lists), wgt_sb[:, h * GW : (h + 1) * GW], ALU.mult)
+
+        x_woven = [keep.tile([P, QW * PACK], BF16, name="x_woven%d" % q, align_bytes=64) for q in range(NQ)]
+
+        def weave_x(q, eng):
+            h, lo = divmod(q * QW, GW)
+            src = planes_walk(picked[h][:, :, lo : lo + QW])
+            if eng == "v":
+                nc.vector.tensor_copy(out=woven_walk(x_woven[q][:]), in_=src)
+            else:
+                nc.scalar.copy(out=woven_walk(x_woven[q][:]), in_=src)
+
+        def quant_x(q):
+            quantize(xg[q], allq, x_woven[q][:])
+            for u in range(2):
+                for v in range(2):
+                    t = 2 * u + v
+                    mx_pass(acc[q, u][:, v, :], wtq, slice(t * P, (t + 1) * P), xg[q], allq, False, v == 1)
+
+        y_rows = out_0.rearrange("(p t) j -> p t j", t=PACK)
+        y_words = out_1[0].rearrange("p j i -> p (j i)").bitcast(I32)
+        y_sb = [keep.tile([P, PACK, QW], F32, name="y_sb%d" % q) for q in range(NQ)]
+        y_woven = [keep.tile([P, QW * PACK], BF16, name="y_woven%d" % q, align_bytes=64) for q in range(NQ)]
+
+        def finish(q):
+            for t in range(PACK):
+                nc.scalar.activation(
+                    out=y_sb[q][:, t, :], in_=acc[q, t // 2][:, t % 2, :], func=ACT.Silu, bias=bias[:, t : t + 1]
+                )
+            nc.sync.dma_start(out=y_rows[:, :, q * QW : (q + 1) * QW], in_=y_sb[q][:])
+
+        def weave_y(q, eng):
+            if eng == "v":
+                nc.vector.tensor_copy(out=woven_walk(y_woven[q][:]), in_=planes_walk(y_sb[q][:]))
+            else:
+                nc.scalar.copy(out=woven_walk(y_woven[q][:]), in_=planes_walk(y_sb[q][:]))
+
+        def quant_y(q):
+            cols = slice(q * QW, (q + 1) * QW)
+            quantize(yq, cols, y_woven[q][:])
+            nc.sync.dma_start(out=y_words[:, cols], in_=yq[0][:, cols].bitcast(I32))
+
+        c_first(0)
+        c_first(1)
+        c_second(0)
+        c_second(1)
+        make_wt()
+        c_first(2)
+        c_first(3)
+        make_wx()
+        c_second(2)
+        c_second(3)
+        for q in range(NQ):
+            tier_passes(q)
+        for t in range(PACK):
+            gather(t, 0)
+            gather(t, 1)
+        weave_x(0, "s")
+        weave_x(1, "v")
+        quant_x(0)
+        weave_x(2, "s")
+        quant_x(1)
+        finish(0)
+        weave_x(3, "v")
+        quant_x(2)
+        finish(1)
+        quant_x(3)
+        weave_y(0, "s")
+        finish(2)
+        finish(3)
+        quant_y(0)
+        weave_y(1, "v")
+        weave_y(2, "v")
+        quant_y(1)
+        weave_y(3, "v")
+        quant_y(2)
+        quant_y(3)
+        for Q in range(4):
+            eng = nc.scalar if Q % 2 else nc.sync
+            eng.dma_start(
+                out=out_2[0, 4 * Q : 4 * Q + 4, :].bitcast(I32),
+                in_=yq[1][32 * Q : 32 * Q + 4, :].bitcast(I32),
+            )

@@ -60,62 +60,80 @@ def tile_list_siluP_kernel(
         c_rows = c.rearrange("(p t) j -> p t j", t=PACK)
         x_planes = xT.rearrange("(p t) s -> t p s", t=PACK)
         c_raw = []
+        c_all = keep.tile([P, PACK * J], F32, name="c_all", tag="c_all")
         def load_c(lo, hi):
-            tl = keep.tile([P, PACK, hi - lo], F32, name="c_raw%d" % lo)
-            nc.sync.dma_start(out=tl[:], in_=c_rows[:, :, lo:hi])
-            for q0 in range(lo, hi, QW):
-                c_raw.append(tl[:, :, q0 - lo : q0 - lo + QW])
+            part = c_all[:, lo * PACK : hi * PACK].rearrange("p (t j) -> p t j", t=PACK)
+            nc.sync.dma_start(out=part, in_=c_rows[:, :, lo:hi])
+            c_raw.append(part)
         wt_raw = keep.tile([P, PACK, N], F32)
         wxw_raw = keep.tile([P, N], I32)
         wxs_raw = keep.tile([P, N], U8)
         offsets = keep.tile([P, J // 16], U16)
         wgt_sb = keep.tile([P, J], F32)
         bias = keep.tile([P, PACK], F32)
-        x_sb = [keep.tile([P, T], F32, name="x_plane%d" % t) for t in range(PACK)]
-        nc.gpsimd.memset(wxs_raw[:].bitcast(I32), 0)
+        x_sb = [keep.tile([P, T], F32, name="x_plane%d" % t, tag="x_plane%d" % t, align_bytes=64) for t in range(PACK)]
+        nc.vector.memset(wxs_raw[:].bitcast(I32), 0)
         load_c(0, 256)
         load_c(256, 512)
         for Q in range(4):
             nc.sync.dma_start(out=wxs_raw[32 * Q : 32 * Q + 4, :].bitcast(I32), in_=wx_scales[0, 4 * Q : 4 * Q + 4, :].bitcast(I32))
-        nc.sync.dma_start(out=wt_raw[:], in_=wt.rearrange("(p j) n -> p j n", j=PACK))
-        load_c(512, 1024)
+        load_c(512, 768)
+        load_c(768, 1024)
         nc.sync.dma_start(out=wxw_raw[:], in_=wx_words[0].rearrange("p n i -> p (n i)").bitcast(I32))
         nc.sync.dma_start(offsets[:], offs)
         nc.sync.dma_start(out=wgt_sb[:], in_=wgt)
         nc.sync.dma_start(out=x_sb[0][:], in_=x_planes[0])
-        nc.sync.dma_start(out=bias[:], in_=b.rearrange("(p t) -> p t", t=PACK))
         nc.sync.dma_start(out=x_sb[1][:], in_=x_planes[1])
+        nc.sync.dma_start(out=wt_raw[:], in_=wt.rearrange("(p j) n -> p j n", j=PACK))
+        nc.sync.dma_start(out=bias[:], in_=b.rearrange("(p t) -> p t", t=PACK))
         nc.sync.dma_start(out=x_sb[2][:], in_=x_planes[2])
         nc.sync.dma_start(out=x_sb[3][:], in_=x_planes[3])
 
-        ramp = keep.tile([P, P], F32)
-        nc.gpsimd.iota(ramp[:], pattern=[[1, P]], base=0, channel_multiplier=-1, allow_small_or_imprecise_dtypes=True)
+        warm = keep.tile([P, 8], F32)
+        nc.vector.memset(warm[:, 0:1], 0.0)
+        nc.scalar.activation(out=warm[:, 4:5], in_=warm[:, 0:1], func=ACT.Silu)
+        ones = keep.tile([P, 32], F32)
+        along = keep.tile([P, 32], F32, align_bytes=64)
+        down = keep.tile([P, 32], F32, align_bytes=64)
         ident_bf = keep.tile([P, PACK * (P * PACK + 1)], BF16, align_bytes=64)
+        nc.vector.memset(ones[:], 1.0)
         nc.vector.memset(ident_bf[:].bitcast(I32), 0)
-        nc.vector.tensor_scalar(
-            out=ident_bf[:].rearrange("p (t r) -> p t r", t=PACK)[:, :, 0 : P * PACK : PACK],
-            in0=ramp[:].unsqueeze(1).to_broadcast([P, PACK, P]),
-            scalar1=0.0,
-            scalar2=None,
-            op0=ALU.is_equal,
-        )
+        nc.vector.tensor_tensor_scan(along[:], ones[:], ones[:], 0.0, ALU.mult, ALU.add)
+        nc.vector.transpose(down[:], along[:])
+        diagonal = ident_bf[:].rearrange("p (t r) -> p t r", t=PACK)[:, :, 0 : P * PACK : PACK]
+        for Q in range(4):
+            rows = slice(32 * Q, 32 * Q + 32)
+            nc.vector.tensor_tensor(
+                out=diagonal[rows, :, rows],
+                in0=along[rows, :].unsqueeze(1).to_broadcast([32, PACK, 32]),
+                in1=down[rows, :].unsqueeze(1).to_broadcast([32, PACK, 32]),
+                op=ALU.is_equal,
+            )
         ident = operand("ident", PACK * P)
         quantize(ident, slice(0, PACK * P), ident_bf[:, 0 : PACK * P * PACK])
         cq = [operand("cq%d" % q, QW) for q in range(NQ)]
         cr = [operand("cr%d" % q, QW) for q in range(NQ)]
-        xg = [operand("xg%d" % q, QW) for q in range(NQ)]
         wtq = operand("wt", N)
-        wxq = operand("wx", N)
+        wxq = []
         yq = operand("y", J)
         allq = slice(0, QW)
 
-        def c_first(q):
-            woven = keep.tile([P, QW * PACK], BF16, name="c_woven%d" % q, align_bytes=64)
-            nc.scalar.copy(out=woven_walk(woven[:]), in_=planes_walk(c_raw[q]))
+        cw = {}
+
+        def c_first(q, eng="s"):
+            woven = keep.tile([P, QW * PACK], BF16, name="c_woven%d" % q, tag="c_woven%d" % q, align_bytes=64)
+            cw[q] = woven
+            if eng == "v":
+                nc.vector.tensor_copy(out=woven_walk(woven[:]), in_=planes_walk(c_raw[q]))
+            else:
+                nc.scalar.copy(out=woven_walk(woven[:]), in_=planes_walk(c_raw[q]))
             quantize(cq[q], allq, woven[:])
+
+        rw = {}
 
         def c_second(q):
             woven = keep.tile([P, QW * PACK], BF16, name="r_woven%d" % q, align_bytes=64)
+            rw[q] = woven
             for u in range(2):
                 cols = slice(u * P, (u + 1) * P)
                 back = psum.tile([P, PACK, P], F32, name="back%d_%d" % (q, u), tag="bank%d" % (2 * q + u))
@@ -130,7 +148,7 @@ def tile_list_siluP_kernel(
             quantize(cr[q], allq, woven[:])
 
         def make_wt():
-            woven = keep.tile([P, N * PACK], BF16, name="wt_woven", align_bytes=64)
+            woven = keep.tile([P, N * PACK], BF16, name="wt_woven", tag="x_plane0", align_bytes=64)
             nc.scalar.copy(
                 out=woven[:].rearrange("p (t m j) -> p m j t", t=PACK, j=PACK),
                 in_=wt_raw[:].rearrange("p j (m t) -> p m j t", t=PACK),
@@ -138,6 +156,8 @@ def tile_list_siluP_kernel(
             quantize(wtq, slice(0, N), woven[:])
 
         def make_wx():
+            wxq.append(keep.tile([P, N], U32, name="wx_codes", tag="c_woven3", align_bytes=64))
+            wxq.append(keep.tile([P, N], U8, name="wx_scale", tag="c_woven2", align_bytes=64))
             nc.vector.tensor_copy(
                 out=wxq[0][:].bitcast(I32).rearrange("p (t h m) -> p h t m", t=PACK, m=4),
                 in_=wxw_raw[:].rearrange("p (h m t) -> p h t m", t=PACK, m=4),
@@ -147,98 +167,144 @@ def tile_list_siluP_kernel(
                 in_=wxs_raw[:].rearrange("p (m t) -> p t m", t=PACK),
             )
 
+        units = [128,128,256,256,128,128]
+        starts = [sum(units[:u]) for u in range(len(units))]
         acc = {}
 
-        def tier_passes(q):
-            for u in range(2):
-                acc[q, u] = psum.tile([P, 2, QW], F32, name="acc%d_%d" % (q, u), tag="bank%d" % (2 * q + u))
-                for v in range(2):
-                    t = 2 * u + v
-                    mx_pass(acc[q, u][:, v, :], wxq, slice(t * P, (t + 1) * P), cq[q], allq, v == 0, False)
-                    mx_pass(acc[q, u][:, v, :], wxq, slice(t * P, (t + 1) * P), cr[q], allq, False, False)
+        def ucols(u):
+            return slice(starts[u], starts[u] + units[u])
 
-        GW = 512
-        picked = [keep.tile([P, PACK, GW], F32, name="picked%d" % h) for h in range(J // GW)]
+        def tier_passes(u):
+            w = units[u]
+            per_bank = 512 // w
+            q, lo = divmod(starts[u], QW)
+            for t in range(PACK):
+                if t % per_bank == 0:
+                    bank = psum.tile([P, per_bank, w], F32, name="acc%d_%d" % (u, t), tag="bank%d" % (starts[u] // P + t // per_bank))
+                acc[u, t] = bank[:, t % per_bank, :]
+                mx_pass(acc[u, t], wxq, slice(t * P, (t + 1) * P), cq[q], slice(lo, lo + w), t % per_bank == 0, False)
+                mx_pass(acc[u, t], wxq, slice(t * P, (t + 1) * P), cr[q], slice(lo, lo + w), False, False)
 
-        def gather(t, h):
-            lists = offsets[:, h * GW // 16 : (h + 1) * GW // 16]
-            nc.vector.tensor_tensor(picked[h][:, t, :], x_sb[t][:].indirect(lists), wgt_sb[:, h * GW : (h + 1) * GW], ALU.mult)
+        picked = []
 
-        x_woven = [keep.tile([P, QW * PACK], BF16, name="x_woven%d" % q, align_bytes=64) for q in range(NQ)]
+        def open_picked():
+            flat = keep.tile([P, PACK * J], F32, name="picked", tag="c_all")
+            for h in range(2):
+                picked.append(flat[:, h * PACK * HALF : (h + 1) * PACK * HALF].rearrange("p (t j) -> p t j", t=PACK))
 
-        def weave_x(q, eng):
-            h, lo = divmod(q * QW, GW)
-            src = planes_walk(picked[h][:, :, lo : lo + QW])
+        def picked_part(cols):
+            h = cols.start // HALF
+            return picked[h][:, :, cols.start - h * HALF : cols.stop - h * HALF]
+
+        x_woven = [keep.tile([P, w * PACK], BF16, name="x_woven%d" % u, align_bytes=64) for u, w in enumerate(units)]
+        xu = [operand("xu%d" % u, w) for u, w in enumerate(units)]
+
+        def gather(t, cols):
+            lists = offsets[:, cols.start // 16 : cols.stop // 16]
+            nc.vector.tensor_tensor(picked_part(cols)[:, t, :], x_sb[t][:].indirect(lists), wgt_sb[:, cols], ALU.mult)
+
+        def copy(eng, out, in_):
             if eng == "v":
-                nc.vector.tensor_copy(out=woven_walk(x_woven[q][:]), in_=src)
+                nc.vector.tensor_copy(out=out, in_=in_)
             else:
-                nc.scalar.copy(out=woven_walk(x_woven[q][:]), in_=src)
+                nc.scalar.copy(out=out, in_=in_)
 
-        def quant_x(q):
-            quantize(xg[q], allq, x_woven[q][:])
-            for u in range(2):
-                for v in range(2):
-                    t = 2 * u + v
-                    mx_pass(acc[q, u][:, v, :], wtq, slice(t * P, (t + 1) * P), xg[q], allq, False, v == 1)
+        def weave_x(u, eng):
+            copy(eng, woven_walk(x_woven[u][:]), planes_walk(picked_part(ucols(u))))
+
+        def quant_x(u):
+            w = units[u]
+            per_bank = 512 // w
+            quantize(xu[u], slice(0, w), x_woven[u][:])
+            for t in range(PACK):
+                mx_pass(acc[u, t], wtq, slice(t * P, (t + 1) * P), xu[u], slice(0, w), False, t % per_bank == per_bank - 1)
 
         y_rows = out_0.rearrange("(p t) j -> p t j", t=PACK)
         y_words = out_1[0].rearrange("p j i -> p (j i)").bitcast(I32)
         y_sb = [keep.tile([P, PACK, QW], F32, name="y_sb%d" % q) for q in range(NQ)]
-        y_woven = [keep.tile([P, QW * PACK], BF16, name="y_woven%d" % q, align_bytes=64) for q in range(NQ)]
+        y_woven = [keep.tile([P, w * PACK], BF16, name="y_woven%d" % u, align_bytes=64) for u, w in enumerate(units)]
 
-        def finish(q):
+        def y_part(lo, hi):
+            q = lo // QW
+            return y_sb[q][:, :, lo - q * QW : hi - q * QW]
+
+        def finish(u):
+            y = y_part(starts[u], starts[u] + units[u])
             for t in range(PACK):
-                nc.scalar.activation(
-                    out=y_sb[q][:, t, :], in_=acc[q, t // 2][:, t % 2, :], func=ACT.Silu, bias=bias[:, t : t + 1]
-                )
-            nc.sync.dma_start(out=y_rows[:, :, q * QW : (q + 1) * QW], in_=y_sb[q][:])
+                nc.scalar.activation(out=y[:, t, :], in_=acc[u, t], func=ACT.Silu, bias=bias[:, t : t + 1])
 
-        def weave_y(q, eng):
-            if eng == "v":
-                nc.vector.tensor_copy(out=woven_walk(y_woven[q][:]), in_=planes_walk(y_sb[q][:]))
-            else:
-                nc.scalar.copy(out=woven_walk(y_woven[q][:]), in_=planes_walk(y_sb[q][:]))
+        def store_y(lo, hi):
+            nc.sync.dma_start(out=y_rows[:, :, lo:hi], in_=y_part(lo, hi))
 
-        def quant_y(q):
-            cols = slice(q * QW, (q + 1) * QW)
-            quantize(yq, cols, y_woven[q][:])
-            nc.sync.dma_start(out=y_words[:, cols], in_=yq[0][:, cols].bitcast(I32))
+        def weave_y(u, eng):
+            copy(eng, woven_walk(y_woven[u][:]), planes_walk(y_part(starts[u], starts[u] + units[u])))
 
-        c_first(0)
+        def quant_y(u):
+            quantize(yq, ucols(u), y_woven[u][:])
+
+        def store_words(lo, hi):
+            nc.sync.dma_start(out=y_words[:, lo:hi], in_=yq[0][:, lo:hi].bitcast(I32))
+
+        c_first(0, "v")
         c_first(1)
         c_second(0)
-        c_second(1)
-        make_wt()
         c_first(2)
+        c_second(1)
         c_first(3)
-        make_wx()
         c_second(2)
         c_second(3)
-        for q in range(NQ):
-            tier_passes(q)
-        for t in range(PACK):
-            gather(t, 0)
-            gather(t, 1)
+        make_wx()
+        for u in range(len(units)):
+            tier_passes(u)
+        open_picked()
+        for t in range(3):
+            if t == 2:
+                make_wt()
+            gather(t, slice(0, HALF))
+            gather(t, slice(HALF, J))
+        gather(3, ucols(0))
         weave_x(0, "s")
-        weave_x(1, "v")
+        gather(3, ucols(1))
+        weave_x(1, "s")
         quant_x(0)
+        gather(3, ucols(2))
         weave_x(2, "s")
         quant_x(1)
         finish(0)
-        weave_x(3, "v")
+        gather(3, ucols(3))
         quant_x(2)
         finish(1)
+        store_y(0, 256)
+        gather(3, ucols(4))
+        weave_x(3, "v")
+        gather(3, ucols(5))
         quant_x(3)
-        weave_y(0, "s")
+        weave_x(4, "v")
+        weave_x(5, "v")
+        quant_x(4)
         finish(2)
-        finish(3)
-        quant_y(0)
+        store_y(256, 512)
+        quant_x(5)
+        weave_y(0, "v")
         weave_y(1, "v")
-        weave_y(2, "v")
+        finish(3)
+        store_y(512, 768)
+        quant_y(0)
         quant_y(1)
+        weave_y(2, "v")
+        finish(4)
+        store_y(768, 896)
+        finish(5)
+        store_y(896, 1024)
         weave_y(3, "v")
         quant_y(2)
         quant_y(3)
+        store_words(0, 768)
+        weave_y(4, "v")
+        weave_y(5, "v")
+        quant_y(4)
+        quant_y(5)
+        store_words(768, 1024)
         for Q in range(4):
             eng = nc.scalar if Q % 2 else nc.sync
             eng.dma_start(

@@ -81,13 +81,13 @@ def tile_list_siluP_kernel(
         load_c(768, 1024)
         nc.sync.dma_start(out=wxw_raw[:], in_=wx_words[0].rearrange("p n i -> p (n i)").bitcast(I32))
         nc.sync.dma_start(offsets[:], offs)
-        nc.sync.dma_start(out=wgt_sb[:], in_=wgt)
         nc.sync.dma_start(out=x_sb[0][:], in_=x_planes[0])
         nc.sync.dma_start(out=x_sb[1][:], in_=x_planes[1])
         nc.sync.dma_start(out=wt_raw[:], in_=wt.rearrange("(p j) n -> p j n", j=PACK))
         nc.sync.dma_start(out=bias[:], in_=b.rearrange("(p t) -> p t", t=PACK))
         nc.sync.dma_start(out=x_sb[2][:], in_=x_planes[2])
         nc.sync.dma_start(out=x_sb[3][:], in_=x_planes[3])
+        nc.sync.dma_start(out=wgt_sb[:], in_=wgt)
 
         warm = keep.tile([P, 8], F32)
         nc.vector.memset(warm[:, 0:1], 0.0)
@@ -95,7 +95,7 @@ def tile_list_siluP_kernel(
         ones = keep.tile([P, 32], F32)
         along = keep.tile([P, 32], F32, align_bytes=64)
         down = keep.tile([P, 32], F32, align_bytes=64)
-        ident_bf = keep.tile([P, PACK * (P * PACK + 1)], BF16, align_bytes=64)
+        ident_bf = keep.tile([P, PACK * (P * PACK + 1)], BF16, name="ident_bf", tag="staging", align_bytes=64)
         nc.vector.memset(ones[:], 1.0)
         nc.vector.memset(ident_bf[:].bitcast(I32), 0)
         nc.vector.tensor_tensor_scan(along[:], ones[:], ones[:], 0.0, ALU.mult, ALU.add)
@@ -118,21 +118,20 @@ def tile_list_siluP_kernel(
         yq = operand("y", J)
         allq = slice(0, QW)
 
-        cw = {}
+        c_woven = keep.tile([P, J * PACK], BF16, name="c_woven", tag="staging", align_bytes=64)
 
         def c_first(q, eng="s"):
-            woven = keep.tile([P, QW * PACK], BF16, name="c_woven%d" % q, tag="c_woven%d" % q, align_bytes=64)
-            cw[q] = woven
+            woven = c_woven[:, q * QW * PACK : (q + 1) * QW * PACK]
             if eng == "v":
-                nc.vector.tensor_copy(out=woven_walk(woven[:]), in_=planes_walk(c_raw[q]))
+                nc.vector.tensor_copy(out=woven_walk(woven), in_=planes_walk(c_raw[q]))
             else:
-                nc.scalar.copy(out=woven_walk(woven[:]), in_=planes_walk(c_raw[q]))
-            quantize(cq[q], allq, woven[:])
+                nc.scalar.copy(out=woven_walk(woven), in_=planes_walk(c_raw[q]))
+            quantize(cq[q], allq, woven)
 
         rw = {}
 
         def c_second(q):
-            woven = keep.tile([P, QW * PACK], BF16, name="r_woven%d" % q, align_bytes=64)
+            woven = keep.tile([P, QW * PACK], BF16, name="r_woven%d" % q, tag="r_woven%d" % q, align_bytes=64)
             rw[q] = woven
             for u in range(2):
                 cols = slice(u * P, (u + 1) * P)
@@ -156,8 +155,8 @@ def tile_list_siluP_kernel(
             quantize(wtq, slice(0, N), woven[:])
 
         def make_wx():
-            wxq.append(keep.tile([P, N], U32, name="wx_codes", tag="c_woven3", align_bytes=64))
-            wxq.append(keep.tile([P, N], U8, name="wx_scale", tag="c_woven2", align_bytes=64))
+            wxq.append(keep.tile([P, N], U32, name="wx_codes", tag="staging", align_bytes=64))
+            wxq.append(keep.tile([P, N], U8, name="wx_scale", tag="r_woven0", align_bytes=64))
             nc.vector.tensor_copy(
                 out=wxq[0][:].bitcast(I32).rearrange("p (t h m) -> p h t m", t=PACK, m=4),
                 in_=wxw_raw[:].rearrange("p (h m t) -> p h t m", t=PACK, m=4),
@@ -167,7 +166,7 @@ def tile_list_siluP_kernel(
                 in_=wxs_raw[:].rearrange("p (m t) -> p t m", t=PACK),
             )
 
-        units = [128,128,256,256,128,128]
+        units = [256,256,256,128,128]
         starts = [sum(units[:u]) for u in range(len(units))]
         acc = {}
 
@@ -201,7 +200,7 @@ def tile_list_siluP_kernel(
 
         def gather(t, cols):
             lists = offsets[:, cols.start // 16 : cols.stop // 16]
-            nc.vector.tensor_tensor(picked_part(cols)[:, t, :], x_sb[t][:].indirect(lists), wgt_sb[:, cols], ALU.mult)
+            nc.vector.tensor_copy(picked_part(cols)[:, t, :], x_sb[t][:].indirect(lists))
 
         def copy(eng, out, in_):
             if eng == "v":
@@ -210,7 +209,13 @@ def tile_list_siluP_kernel(
                 nc.scalar.copy(out=out, in_=in_)
 
         def weave_x(u, eng):
-            copy(eng, woven_walk(x_woven[u][:]), planes_walk(picked_part(ucols(u))))
+            w = wgt_sb[:, ucols(u)].rearrange("p (c i) -> p c i", i=4)
+            nc.vector.tensor_tensor(
+                out=woven_walk(x_woven[u][:]),
+                in0=planes_walk(picked_part(ucols(u))),
+                in1=w.unsqueeze(2).to_broadcast([P, units[u] // 4, PACK, 4]),
+                op=ALU.mult,
+            )
 
         def quant_x(u):
             w = units[u]
@@ -262,48 +267,39 @@ def tile_list_siluP_kernel(
                 make_wt()
             gather(t, slice(0, HALF))
             gather(t, slice(HALF, J))
-        gather(3, ucols(0))
-        weave_x(0, "s")
-        gather(3, ucols(1))
-        weave_x(1, "s")
+        gather(3, slice(0, HALF))
+        weave_x(0, "v")
+        gather(3, slice(HALF, J))
         quant_x(0)
-        gather(3, ucols(2))
-        weave_x(2, "s")
-        quant_x(1)
+        weave_x(1, "v")
         finish(0)
-        gather(3, ucols(3))
+        store_y(0, 256)
+        weave_x(2, "v")
+        quant_x(1)
+        weave_y(0, "s")
+        weave_x(3, "v")
         quant_x(2)
         finish(1)
-        store_y(0, 256)
-        gather(3, ucols(4))
-        weave_x(3, "v")
-        gather(3, ucols(5))
-        quant_x(3)
+        store_y(256, 512)
         weave_x(4, "v")
-        weave_x(5, "v")
+        quant_x(3)
         quant_x(4)
         finish(2)
-        store_y(256, 512)
-        quant_x(5)
-        weave_y(0, "v")
-        weave_y(1, "v")
-        finish(3)
         store_y(512, 768)
         quant_y(0)
-        quant_y(1)
-        weave_y(2, "v")
-        finish(4)
+        weave_y(1, "v")
+        finish(3)
         store_y(768, 896)
-        finish(5)
+        finish(4)
         store_y(896, 1024)
-        weave_y(3, "v")
+        weave_y(2, "v")
+        quant_y(1)
         quant_y(2)
-        quant_y(3)
         store_words(0, 768)
+        weave_y(3, "v")
         weave_y(4, "v")
-        weave_y(5, "v")
+        quant_y(3)
         quant_y(4)
-        quant_y(5)
         store_words(768, 1024)
         for Q in range(4):
             eng = nc.scalar if Q % 2 else nc.sync

@@ -17,17 +17,28 @@ ACT = mybir.ActivationFunctionType
 
 P = 128
 PACK = 4
-QW = 256
-NQ = J // QW
-HALF = 512
+LINE = 4
+BANK = 512
+GROUP = 16
+QUADRANTS = 4
+QUARTER = J // 4
+HALF = J // 2
+UNITS = (256, 256, 256, 128, 128)
+STARTS = tuple(sum(UNITS[:u]) for u in range(len(UNITS)))
+WOVEN_ON_VECTOR = (2, 4)
+WIDE_UNITS = 3
 
 
-def planes_walk(ap):
-    return ap.rearrange("p t (c i) -> p c t i", i=4)
+def planes_walk(planes):
+    return planes.rearrange("p t (c i) -> p c t i", i=LINE)
 
 
-def woven_walk(ap):
-    return ap.rearrange("p (c i t) -> p c t i", i=4, t=PACK)
+def woven_walk(woven):
+    return woven.rearrange("p (c i t) -> p c t i", i=LINE, t=PACK)
+
+
+def span(start, width):
+    return slice(start, start + width)
 
 
 def tile_list_siluP_kernel(
@@ -43,267 +54,230 @@ def tile_list_siluP_kernel(
             scales = keep.tile([P, width], U8, name=name + "_scales", align_bytes=64)
             return codes, scales
 
-        def quantize(op, cols, woven):
-            nc.vector.quantize_mx(out=op[0][:, cols].bitcast(FP8X4), scales=op[1][:, cols], in_=woven)
+        def quantize(target, cols, woven):
+            codes, scales = target
+            nc.vector.quantize_mx(out=codes[:, cols].bitcast(FP8X4), scales=scales[:, cols], in_=woven)
 
-        def mx_pass(out, stat, stat_cols, mov, mov_cols, start, stop):
+        def mx_pass(out, weights, t, moving, cols, start, stop):
             nc.tensor.matmul_mx(
                 out=out,
-                lhsT=stat[0][:, stat_cols].bitcast(FP8X4),
-                lhsT_scale=stat[1][:, stat_cols],
-                rhs=mov[0][:, mov_cols].bitcast(FP8X4),
-                rhs_scale=mov[1][:, mov_cols],
+                lhsT=weights[0][:, span(t * P, P)].bitcast(FP8X4),
+                lhsT_scale=weights[1][:, span(t * P, P)],
+                rhs=moving[0][:, cols].bitcast(FP8X4),
+                rhs_scale=moving[1][:, cols],
                 start=start,
                 stop=stop,
             )
 
-        c_rows = c.rearrange("(p t) j -> p t j", t=PACK)
-        x_planes = xT.rearrange("(p t) s -> t p s", t=PACK)
-        c_raw = []
-        c_all = keep.tile([P, PACK * J], F32, name="c_all", tag="c_all")
-        def load_c(lo, hi):
-            part = c_all[:, lo * PACK : hi * PACK].rearrange("p (t j) -> p t j", t=PACK)
-            nc.sync.dma_start(out=part, in_=c_rows[:, :, lo:hi])
-            c_raw.append(part)
+        def weave(on_vector, woven, planes):
+            if on_vector:
+                nc.vector.tensor_copy(out=woven_walk(woven), in_=planes_walk(planes))
+            else:
+                nc.scalar.copy(out=woven_walk(woven), in_=planes_walk(planes))
+
+        c_all = keep.tile([P, PACK * J], F32, name="c_all", tag="c_then_picked")
+        c_planes = [
+            c_all[:, span(q * PACK * QUARTER, PACK * QUARTER)].rearrange("p (t j) -> p t j", t=PACK)
+            for q in range(J // QUARTER)
+        ]
         wt_raw = keep.tile([P, PACK, N], F32)
-        wxw_raw = keep.tile([P, N], I32)
-        wxs_raw = keep.tile([P, N], U8)
-        offsets = keep.tile([P, J // 16], U16)
+        wx_words_raw = keep.tile([P, N], I32)
+        wx_scales_raw = keep.tile([P, N], U8)
+        offsets = keep.tile([P, J // GROUP], U16)
         wgt_sb = keep.tile([P, J], F32)
         bias = keep.tile([P, PACK], F32)
-        x_sb = [keep.tile([P, T], F32, name="x_plane%d" % t, tag="x_plane%d" % t, align_bytes=64) for t in range(PACK)]
-        nc.vector.memset(wxs_raw[:].bitcast(I32), 0)
-        load_c(0, 256)
-        load_c(256, 512)
-        for Q in range(4):
-            nc.sync.dma_start(out=wxs_raw[32 * Q : 32 * Q + 4, :].bitcast(I32), in_=wx_scales[0, 4 * Q : 4 * Q + 4, :].bitcast(I32))
-        load_c(512, 768)
-        load_c(768, 1024)
-        nc.sync.dma_start(out=wxw_raw[:], in_=wx_words[0].rearrange("p n i -> p (n i)").bitcast(I32))
+        x_planes = [
+            keep.tile([P, T], F32, name="x_plane%d" % t, tag="x_plane%d" % t, align_bytes=64) for t in range(PACK)
+        ]
+
+        def load_c(q):
+            rows = c.rearrange("(p t) j -> p t j", t=PACK)
+            nc.sync.dma_start(out=c_planes[q], in_=rows[:, :, span(q * QUARTER, QUARTER)])
+
+        def load_x(t):
+            nc.sync.dma_start(out=x_planes[t][:], in_=xT.rearrange("(p t) s -> t p s", t=PACK)[t])
+
+        nc.vector.memset(wx_scales_raw[:].bitcast(I32), 0)
+        load_c(0)
+        load_c(1)
+        for quadrant in range(QUADRANTS):
+            nc.sync.dma_start(
+                out=wx_scales_raw[span(32 * quadrant, 4), :].bitcast(I32),
+                in_=wx_scales[0, span(4 * quadrant, 4), :].bitcast(I32),
+            )
+        load_c(2)
+        load_c(3)
+        nc.sync.dma_start(out=wx_words_raw[:], in_=wx_words[0].rearrange("p n i -> p (n i)").bitcast(I32))
         nc.sync.dma_start(offsets[:], offs)
-        nc.sync.dma_start(out=x_sb[0][:], in_=x_planes[0])
-        nc.sync.dma_start(out=x_sb[1][:], in_=x_planes[1])
-        nc.sync.dma_start(out=wt_raw[:], in_=wt.rearrange("(p j) n -> p j n", j=PACK))
-        nc.sync.dma_start(out=bias[:], in_=b.rearrange("(p t) -> p t", t=PACK))
-        nc.sync.dma_start(out=x_sb[2][:], in_=x_planes[2])
-        nc.sync.dma_start(out=x_sb[3][:], in_=x_planes[3])
         nc.sync.dma_start(out=wgt_sb[:], in_=wgt)
+        load_x(0)
+        load_x(1)
+        nc.sync.dma_start(out=wt_raw[:], in_=wt.rearrange("(p i) n -> p i n", i=PACK))
+        nc.sync.dma_start(out=bias[:], in_=b.rearrange("(p t) -> p t", t=PACK))
+        load_x(2)
+        load_x(3)
 
         warm = keep.tile([P, 8], F32)
         nc.vector.memset(warm[:, 0:1], 0.0)
         nc.scalar.activation(out=warm[:, 4:5], in_=warm[:, 0:1], func=ACT.Silu)
-        ones = keep.tile([P, 32], F32)
-        along = keep.tile([P, 32], F32, align_bytes=64)
-        down = keep.tile([P, 32], F32, align_bytes=64)
-        ident_bf = keep.tile([P, PACK * (P * PACK + 1)], BF16, name="ident_bf", tag="staging", align_bytes=64)
-        nc.vector.memset(ones[:], 1.0)
-        nc.vector.memset(ident_bf[:].bitcast(I32), 0)
-        nc.vector.tensor_tensor_scan(along[:], ones[:], ones[:], 0.0, ALU.mult, ALU.add)
-        nc.vector.transpose(down[:], along[:])
-        diagonal = ident_bf[:].rearrange("p (t r) -> p t r", t=PACK)[:, :, 0 : P * PACK : PACK]
-        for Q in range(4):
-            rows = slice(32 * Q, 32 * Q + 32)
-            nc.vector.tensor_tensor(
-                out=diagonal[rows, :, rows],
-                in0=along[rows, :].unsqueeze(1).to_broadcast([32, PACK, 32]),
-                in1=down[rows, :].unsqueeze(1).to_broadcast([32, PACK, 32]),
-                op=ALU.is_equal,
-            )
-        ident = operand("ident", PACK * P)
-        quantize(ident, slice(0, PACK * P), ident_bf[:, 0 : PACK * P * PACK])
-        cq = [operand("cq%d" % q, QW) for q in range(NQ)]
-        cr = [operand("cr%d" % q, QW) for q in range(NQ)]
-        wtq = operand("wt", N)
-        wxq = []
-        yq = operand("y", J)
-        allq = slice(0, QW)
 
-        c_woven = keep.tile([P, J * PACK], BF16, name="c_woven", tag="staging", align_bytes=64)
+        ramp = keep.tile([P, P], F32)
+        nc.gpsimd.iota(ramp[:], pattern=[[1, P]], base=0, channel_multiplier=-1, allow_small_or_imprecise_dtypes=True)
+        ident_woven = keep.tile([P, PACK * (L + 1)], BF16, name="ident_woven", tag="staging", align_bytes=64)
+        nc.vector.memset(ident_woven[:].bitcast(I32), 0)
+        nc.vector.tensor_scalar(
+            out=ident_woven[:].rearrange("p (t r) -> p t r", t=PACK)[:, :, 0:L:PACK],
+            in0=ramp[:].unsqueeze(1).to_broadcast([P, PACK, P]),
+            scalar1=0.0,
+            scalar2=None,
+            op0=ALU.is_equal,
+        )
+        ident = operand("ident", L)
+        quantize(ident, slice(0, L), ident_woven[:, 0 : PACK * L])
 
-        def c_first(q, eng="s"):
-            woven = c_woven[:, q * QW * PACK : (q + 1) * QW * PACK]
-            if eng == "v":
-                nc.vector.tensor_copy(out=woven_walk(woven), in_=planes_walk(c_raw[q]))
-            else:
-                nc.scalar.copy(out=woven_walk(woven), in_=planes_walk(c_raw[q]))
-            quantize(cq[q], allq, woven)
+        c_q = [operand("c_q%d" % q, QUARTER) for q in range(J // QUARTER)]
+        c_r = [operand("c_r%d" % q, QUARTER) for q in range(J // QUARTER)]
+        c_woven = keep.tile([P, PACK * J], BF16, name="c_woven", tag="staging", align_bytes=64)
 
-        rw = {}
+        def first_tier(q):
+            woven = c_woven[:, span(q * PACK * QUARTER, PACK * QUARTER)]
+            weave(q == 0, woven, c_planes[q])
+            quantize(c_q[q], slice(0, QUARTER), woven)
 
-        def c_second(q):
-            woven = keep.tile([P, QW * PACK], BF16, name="r_woven%d" % q, tag="r_woven%d" % q, align_bytes=64)
-            rw[q] = woven
-            for u in range(2):
-                cols = slice(u * P, (u + 1) * P)
-                back = psum.tile([P, PACK, P], F32, name="back%d_%d" % (q, u), tag="bank%d" % (2 * q + u))
+        def second_tier(q):
+            woven = keep.tile([P, PACK * QUARTER], BF16, name="r_woven%d" % q, tag="r_woven%d" % q, align_bytes=64)
+            for lo in range(0, QUARTER, P):
+                bank = (q * QUARTER + lo) // P
+                back = psum.tile([P, PACK, P], F32, name="back%d" % bank, tag="bank%d" % bank)
                 for t in range(PACK):
-                    mx_pass(back[:, t, :], ident, slice(t * P, (t + 1) * P), cq[q], cols, True, True)
+                    mx_pass(back[:, t, :], ident, t, c_q[q], span(lo, P), True, True)
                 nc.vector.tensor_tensor(
-                    out=woven_walk(woven[:, u * P * PACK : (u + 1) * P * PACK]),
-                    in0=planes_walk(c_raw[q][:, :, cols]),
+                    out=woven_walk(woven[:, span(lo * PACK, P * PACK)]),
+                    in0=planes_walk(c_planes[q][:, :, span(lo, P)]),
                     in1=planes_walk(back[:]),
                     op=ALU.subtract,
                 )
-            quantize(cr[q], allq, woven[:])
+            quantize(c_r[q], slice(0, QUARTER), woven[:])
 
-        def make_wt():
-            woven = keep.tile([P, N * PACK], BF16, name="wt_woven", tag="x_plane0", align_bytes=64)
-            nc.scalar.copy(
-                out=woven[:].rearrange("p (t m j) -> p m j t", t=PACK, j=PACK),
-                in_=wt_raw[:].rearrange("p j (m t) -> p m j t", t=PACK),
-            )
-            quantize(wtq, slice(0, N), woven[:])
+        first_tier(0)
+        for q in range(J // QUARTER):
+            if q + 1 < J // QUARTER:
+                first_tier(q + 1)
+            second_tier(q)
 
-        def make_wx():
-            wxq.append(keep.tile([P, N], U32, name="wx_codes", tag="staging", align_bytes=64))
-            wxq.append(keep.tile([P, N], U8, name="wx_scale", tag="r_woven0", align_bytes=64))
-            nc.vector.tensor_copy(
-                out=wxq[0][:].bitcast(I32).rearrange("p (t h m) -> p h t m", t=PACK, m=4),
-                in_=wxw_raw[:].rearrange("p (h m t) -> p h t m", t=PACK, m=4),
-            )
-            nc.vector.tensor_copy(
-                out=wxq[1][:].rearrange("p (t m) -> p t m", t=PACK),
-                in_=wxs_raw[:].rearrange("p (m t) -> p t m", t=PACK),
-            )
+        wx_q = (
+            keep.tile([P, N], U32, name="wx_codes", tag="staging", align_bytes=64),
+            keep.tile([P, N], U8, name="wx_scales", tag="r_woven0", align_bytes=64),
+        )
+        nc.vector.tensor_copy(
+            out=wx_q[0][:].bitcast(I32).rearrange("p (t h m) -> p h t m", t=PACK, m=LINE),
+            in_=wx_words_raw[:].rearrange("p (h m t) -> p h t m", t=PACK, m=LINE),
+        )
+        nc.vector.tensor_copy(
+            out=wx_q[1][:].rearrange("p (t m) -> p t m", t=PACK),
+            in_=wx_scales_raw[:].rearrange("p (m t) -> p t m", t=PACK),
+        )
 
-        units = [256,256,256,128,128]
-        starts = [sum(units[:u]) for u in range(len(units))]
-        acc = {}
-
-        def ucols(u):
-            return slice(starts[u], starts[u] + units[u])
-
-        def tier_passes(u):
-            w = units[u]
-            per_bank = 512 // w
-            q, lo = divmod(starts[u], QW)
+        sums = {}
+        for u, width in enumerate(UNITS):
+            per_bank = BANK // width
+            q, lo = divmod(STARTS[u], QUARTER)
             for t in range(PACK):
                 if t % per_bank == 0:
-                    bank = psum.tile([P, per_bank, w], F32, name="acc%d_%d" % (u, t), tag="bank%d" % (starts[u] // P + t // per_bank))
-                acc[u, t] = bank[:, t % per_bank, :]
-                mx_pass(acc[u, t], wxq, slice(t * P, (t + 1) * P), cq[q], slice(lo, lo + w), t % per_bank == 0, False)
-                mx_pass(acc[u, t], wxq, slice(t * P, (t + 1) * P), cr[q], slice(lo, lo + w), False, False)
+                    bank = STARTS[u] // P + t // per_bank
+                    group = psum.tile([P, per_bank, width], F32, name="sum%d" % bank, tag="bank%d" % bank)
+                sums[u, t] = group[:, t % per_bank, :]
+                mx_pass(sums[u, t], wx_q, t, c_q[q], span(lo, width), t % per_bank == 0, False)
+                mx_pass(sums[u, t], wx_q, t, c_r[q], span(lo, width), False, False)
 
-        picked = []
+        picked_all = keep.tile([P, PACK * J], F32, name="picked_all", tag="c_then_picked")
 
-        def open_picked():
-            flat = keep.tile([P, PACK * J], F32, name="picked", tag="c_all")
-            for h in range(2):
-                picked.append(flat[:, h * PACK * HALF : (h + 1) * PACK * HALF].rearrange("p (t j) -> p t j", t=PACK))
-
-        def picked_part(cols):
+        def picked(cols):
             h = cols.start // HALF
-            return picked[h][:, :, cols.start - h * HALF : cols.stop - h * HALF]
-
-        x_woven = [keep.tile([P, w * PACK], BF16, name="x_woven%d" % u, align_bytes=64) for u, w in enumerate(units)]
-        xu = [operand("xu%d" % u, w) for u, w in enumerate(units)]
+            half = picked_all[:, span(h * PACK * HALF, PACK * HALF)].rearrange("p (t j) -> p t j", t=PACK)
+            return half[:, :, cols.start - h * HALF : cols.stop - h * HALF]
 
         def gather(t, cols):
-            lists = offsets[:, cols.start // 16 : cols.stop // 16]
-            nc.vector.tensor_copy(picked_part(cols)[:, t, :], x_sb[t][:].indirect(lists))
+            lists = offsets[:, cols.start // GROUP : cols.stop // GROUP]
+            nc.vector.tensor_tensor(picked(cols)[:, t, :], x_planes[t][:].indirect(lists), wgt_sb[:, cols], ALU.mult)
 
-        def copy(eng, out, in_):
-            if eng == "v":
-                nc.vector.tensor_copy(out=out, in_=in_)
-            else:
-                nc.scalar.copy(out=out, in_=in_)
-
-        def weave_x(u, eng):
-            w = wgt_sb[:, ucols(u)].rearrange("p (c i) -> p c i", i=4)
-            nc.vector.tensor_tensor(
-                out=woven_walk(x_woven[u][:]),
-                in0=planes_walk(picked_part(ucols(u))),
-                in1=w.unsqueeze(2).to_broadcast([P, units[u] // 4, PACK, 4]),
-                op=ALU.mult,
-            )
-
-        def quant_x(u):
-            w = units[u]
-            per_bank = 512 // w
-            quantize(xu[u], slice(0, w), x_woven[u][:])
-            for t in range(PACK):
-                mx_pass(acc[u, t], wtq, slice(t * P, (t + 1) * P), xu[u], slice(0, w), False, t % per_bank == per_bank - 1)
-
-        y_rows = out_0.rearrange("(p t) j -> p t j", t=PACK)
-        y_words = out_1[0].rearrange("p j i -> p (j i)").bitcast(I32)
-        y_sb = [keep.tile([P, PACK, QW], F32, name="y_sb%d" % q) for q in range(NQ)]
-        y_woven = [keep.tile([P, w * PACK], BF16, name="y_woven%d" % u, align_bytes=64) for u, w in enumerate(units)]
-
-        def y_part(lo, hi):
-            q = lo // QW
-            return y_sb[q][:, :, lo - q * QW : hi - q * QW]
-
-        def finish(u):
-            y = y_part(starts[u], starts[u] + units[u])
-            for t in range(PACK):
-                nc.scalar.activation(out=y[:, t, :], in_=acc[u, t], func=ACT.Silu, bias=bias[:, t : t + 1])
-
-        def store_y(lo, hi):
-            nc.sync.dma_start(out=y_rows[:, :, lo:hi], in_=y_part(lo, hi))
-
-        def weave_y(u, eng):
-            copy(eng, woven_walk(y_woven[u][:]), planes_walk(y_part(starts[u], starts[u] + units[u])))
-
-        def quant_y(u):
-            quantize(yq, ucols(u), y_woven[u][:])
-
-        def store_words(lo, hi):
-            nc.sync.dma_start(out=y_words[:, lo:hi], in_=yq[0][:, lo:hi].bitcast(I32))
-
-        c_first(0, "v")
-        c_first(1)
-        c_second(0)
-        c_first(2)
-        c_second(1)
-        c_first(3)
-        c_second(2)
-        c_second(3)
-        make_wx()
-        for u in range(len(units)):
-            tier_passes(u)
-        open_picked()
-        for t in range(3):
-            if t == 2:
-                make_wt()
+        def gather_plane(t):
             gather(t, slice(0, HALF))
             gather(t, slice(HALF, J))
-        gather(3, slice(0, HALF))
-        weave_x(0, "v")
-        gather(3, slice(HALF, J))
-        quant_x(0)
-        weave_x(1, "v")
-        finish(0)
-        store_y(0, 256)
-        weave_x(2, "v")
-        quant_x(1)
-        weave_y(0, "s")
-        weave_x(3, "v")
-        quant_x(2)
-        finish(1)
-        store_y(256, 512)
-        weave_x(4, "v")
-        quant_x(3)
-        quant_x(4)
-        finish(2)
-        store_y(512, 768)
-        quant_y(0)
-        weave_y(1, "v")
-        finish(3)
-        store_y(768, 896)
-        finish(4)
-        store_y(896, 1024)
-        weave_y(2, "v")
-        quant_y(1)
-        quant_y(2)
-        store_words(0, 768)
-        weave_y(3, "v")
-        weave_y(4, "v")
-        quant_y(3)
-        quant_y(4)
-        store_words(768, 1024)
-        for Q in range(4):
-            eng = nc.scalar if Q % 2 else nc.sync
-            eng.dma_start(
-                out=out_2[0, 4 * Q : 4 * Q + 4, :].bitcast(I32),
-                in_=yq[1][32 * Q : 32 * Q + 4, :].bitcast(I32),
+
+        gather_plane(0)
+        gather_plane(1)
+
+        wt_q = operand("wt", N)
+        wt_woven = keep.tile([P, PACK * N], BF16, name="wt_woven", tag="x_plane0", align_bytes=64)
+        nc.scalar.copy(
+            out=wt_woven[:].rearrange("p (t m i) -> p m i t", t=PACK, i=PACK),
+            in_=wt_raw[:].rearrange("p i (m t) -> p m i t", t=PACK),
+        )
+        quantize(wt_q, slice(0, N), wt_woven[:])
+
+        gather_plane(2)
+
+        x_woven = [
+            keep.tile([P, PACK * width], BF16, name="x_woven%d" % u, align_bytes=64) for u, width in enumerate(UNITS)
+        ]
+        xg_q = [operand("xg%d" % u, width) for u, width in enumerate(UNITS)]
+        y_quarters = [keep.tile([P, PACK, QUARTER], F32, name="y%d" % q) for q in range(J // QUARTER)]
+        y_woven = [
+            keep.tile([P, PACK * width], BF16, name="y_woven%d" % u, align_bytes=64) for u, width in enumerate(UNITS)
+        ]
+        y_q = operand("y", J)
+
+        def unit_cols(u):
+            return span(STARTS[u], UNITS[u])
+
+        def y_planes(u):
+            q, lo = divmod(STARTS[u], QUARTER)
+            return y_quarters[q][:, :, span(lo, UNITS[u])]
+
+        def weave_x(u):
+            weave(u in WOVEN_ON_VECTOR, x_woven[u][:], picked(unit_cols(u)))
+
+        def close_sums(u):
+            per_bank = BANK // UNITS[u]
+            quantize(xg_q[u], slice(0, UNITS[u]), x_woven[u][:])
+            for t in range(PACK):
+                mx_pass(sums[u, t], wt_q, t, xg_q[u], slice(0, UNITS[u]), False, t % per_bank == per_bank - 1)
+
+        def finish(u):
+            for t in range(PACK):
+                nc.scalar.activation(out=y_planes(u)[:, t, :], in_=sums[u, t], func=ACT.Silu, bias=bias[:, t : t + 1])
+            rows = out_0.rearrange("(p t) j -> p t j", t=PACK)
+            nc.sync.dma_start(out=rows[:, :, unit_cols(u)], in_=y_planes(u))
+
+        def store_words(cols):
+            words = out_1[0].rearrange("p j i -> p (j i)").bitcast(I32)
+            nc.sync.dma_start(out=words[:, cols], in_=y_q[0][:, cols].bitcast(I32))
+
+        lead = HALF // UNITS[0]
+        for u in range(lead):
+            gather(PACK - 1, unit_cols(u))
+            weave_x(u)
+        gather(PACK - 1, slice(HALF, J))
+        for u in range(len(UNITS) + 1):
+            if u < len(UNITS):
+                close_sums(u)
+            if u + lead < len(UNITS):
+                weave_x(u + lead)
+            if u > 0:
+                finish(u - 1)
+
+        for u in range(len(UNITS) + 1):
+            if u < len(UNITS):
+                weave(True, y_woven[u][:], y_planes(u))
+            if u > 0:
+                quantize(y_q, unit_cols(u - 1), y_woven[u - 1][:])
+            if u == WIDE_UNITS:
+                store_words(slice(0, STARTS[WIDE_UNITS]))
+        store_words(slice(STARTS[WIDE_UNITS], J))
+        for quadrant in range(QUADRANTS):
+            queue = nc.scalar if quadrant % 2 else nc.sync
+            queue.dma_start(
+                out=out_2[0, span(4 * quadrant, 4), :].bitcast(I32),
+                in_=y_q[1][span(32 * quadrant, 4), :].bitcast(I32),
             )

from contextlib import ExitStack

import concourse.mybir as mybir

K, L, N, T, J = 512, 512, 512, 2048, 1024
FLOPS = 2 * N * J * (K + 2 * L) + 2 * L * L * J

F32 = mybir.dt.float32
BF16 = mybir.dt.bfloat16
I32 = mybir.dt.int32
U32 = mybir.dt.uint32
U16 = mybir.dt.uint16
U8 = mybir.dt.uint8
FP8X4 = mybir.dt.float8_e4m3fn_x4
ALU = mybir.AluOpType
ACT = mybir.ActivationFunctionType

P = 128
PACK = 4
LINE = 4
BANK = 512
GROUP = 16
QUADRANTS = 4
QUARTER = J // 4
HALF = J // 2
UNITS = (256, 256, 256, 128, 128)
STARTS = tuple(sum(UNITS[:u]) for u in range(len(UNITS)))
WOVEN_ON_VECTOR = (2, 4)
WIDE_UNITS = 3


def planes_walk(planes):
    return planes.rearrange("p t (c i) -> p c t i", i=LINE)


def woven_walk(woven):
    return woven.rearrange("p (c i t) -> p c t i", i=LINE, t=PACK)


def span(start, width):
    return slice(start, start + width)


def tile_list_siluP_kernel(
    tc, xT, wgt, wt, c, wx_words, wx_scales, b, offs, out_0, out_1, out_2
):
    nc = tc.nc
    with ExitStack() as ctx:
        keep = ctx.enter_context(tc.tile_pool(name="keep", bufs=1))
        psum = ctx.enter_context(tc.psum_pool(name="psum", bufs=1))

        def operand(name, width):
            codes = keep.tile([P, width], U32, name=name + "_codes", align_bytes=64)
            scales = keep.tile([P, width], U8, name=name + "_scales", align_bytes=64)
            return codes, scales

        def quantize(target, cols, woven):
            codes, scales = target
            nc.vector.quantize_mx(out=codes[:, cols].bitcast(FP8X4), scales=scales[:, cols], in_=woven)

        def mx_pass(out, weights, t, moving, cols, start, stop):
            nc.tensor.matmul_mx(
                out=out,
                lhsT=weights[0][:, span(t * P, P)].bitcast(FP8X4),
                lhsT_scale=weights[1][:, span(t * P, P)],
                rhs=moving[0][:, cols].bitcast(FP8X4),
                rhs_scale=moving[1][:, cols],
                start=start,
                stop=stop,
            )

        def weave(on_vector, woven, planes):
            if on_vector:
                nc.vector.tensor_copy(out=woven_walk(woven), in_=planes_walk(planes))
            else:
                nc.scalar.copy(out=woven_walk(woven), in_=planes_walk(planes))

        c_all = keep.tile([P, PACK * J], F32, name="c_all", tag="c_then_picked")
        c_planes = [
            c_all[:, span(q * PACK * QUARTER, PACK * QUARTER)].rearrange("p (t j) -> p t j", t=PACK)
            for q in range(J // QUARTER)
        ]
        wt_raw = keep.tile([P, PACK, N], F32)
        wx_words_raw = keep.tile([P, N], I32)
        wx_scales_raw = keep.tile([P, N], U8)
        offsets = keep.tile([P, J // GROUP], U16)
        wgt_sb = keep.tile([P, J], F32)
        bias = keep.tile([P, PACK], F32)
        x_planes = [
            keep.tile([P, T], F32, name="x_plane%d" % t, tag="x_plane%d" % t, align_bytes=64) for t in range(PACK)
        ]

        def load_c(q):
            rows = c.rearrange("(p t) j -> p t j", t=PACK)
            nc.sync.dma_start(out=c_planes[q], in_=rows[:, :, span(q * QUARTER, QUARTER)])

        def load_x(t):
            nc.sync.dma_start(out=x_planes[t][:], in_=xT.rearrange("(p t) s -> t p s", t=PACK)[t])

        nc.vector.memset(wx_scales_raw[:].bitcast(I32), 0)
        load_c(0)
        load_c(1)
        for quadrant in range(QUADRANTS):
            nc.sync.dma_start(
                out=wx_scales_raw[span(32 * quadrant, 4), :].bitcast(I32),
                in_=wx_scales[0, span(4 * quadrant, 4), :].bitcast(I32),
            )
        load_c(2)
        load_c(3)
        nc.sync.dma_start(out=wx_words_raw[:], in_=wx_words[0].rearrange("p n i -> p (n i)").bitcast(I32))
        nc.sync.dma_start(offsets[:], offs)
        nc.sync.dma_start(out=wgt_sb[:], in_=wgt)
        load_x(0)
        load_x(1)
        nc.sync.dma_start(out=wt_raw[:], in_=wt.rearrange("(p i) n -> p i n", i=PACK))
        nc.sync.dma_start(out=bias[:], in_=b.rearrange("(p t) -> p t", t=PACK))
        load_x(2)
        load_x(3)

        warm = keep.tile([P, 8], F32)
        nc.vector.memset(warm[:, 0:1], 0.0)
        nc.scalar.activation(out=warm[:, 4:5], in_=warm[:, 0:1], func=ACT.Silu)

        ramp = keep.tile([P, P], F32)
        nc.gpsimd.iota(ramp[:], pattern=[[1, P]], base=0, channel_multiplier=-1, allow_small_or_imprecise_dtypes=True)
        ident_woven = keep.tile([P, PACK * (L + 1)], BF16, name="ident_woven", tag="staging", align_bytes=64)
        nc.vector.memset(ident_woven[:].bitcast(I32), 0)
        nc.vector.tensor_scalar(
            out=ident_woven[:].rearrange("p (t r) -> p t r", t=PACK)[:, :, 0:L:PACK],
            in0=ramp[:].unsqueeze(1).to_broadcast([P, PACK, P]),
            scalar1=0.0,
            scalar2=None,
            op0=ALU.is_equal,
        )
        ident = operand("ident", L)
        quantize(ident, slice(0, L), ident_woven[:, 0 : PACK * L])

        c_q = [operand("c_q%d" % q, QUARTER) for q in range(J // QUARTER)]
        c_r = [operand("c_r%d" % q, QUARTER) for q in range(J // QUARTER)]
        c_woven = keep.tile([P, PACK * J], BF16, name="c_woven", tag="staging", align_bytes=64)

        def first_tier(q):
            woven = c_woven[:, span(q * PACK * QUARTER, PACK * QUARTER)]
            weave(q == 0, woven, c_planes[q])
            quantize(c_q[q], slice(0, QUARTER), woven)

        def second_tier(q):
            woven = keep.tile([P, PACK * QUARTER], BF16, name="r_woven%d" % q, tag="r_woven%d" % q, align_bytes=64)
            for lo in range(0, QUARTER, P):
                bank = (q * QUARTER + lo) // P
                back = psum.tile([P, PACK, P], F32, name="back%d" % bank, tag="bank%d" % bank)
                for t in range(PACK):
                    mx_pass(back[:, t, :], ident, t, c_q[q], span(lo, P), True, True)
                nc.vector.tensor_tensor(
                    out=woven_walk(woven[:, span(lo * PACK, P * PACK)]),
                    in0=planes_walk(c_planes[q][:, :, span(lo, P)]),
                    in1=planes_walk(back[:]),
                    op=ALU.subtract,
                )
            quantize(c_r[q], slice(0, QUARTER), woven[:])

        first_tier(0)
        for q in range(J // QUARTER):
            if q + 1 < J // QUARTER:
                first_tier(q + 1)
            second_tier(q)

        wx_q = (
            keep.tile([P, N], U32, name="wx_codes", tag="staging", align_bytes=64),
            keep.tile([P, N], U8, name="wx_scales", tag="r_woven0", align_bytes=64),
        )
        nc.vector.tensor_copy(
            out=wx_q[0][:].bitcast(I32).rearrange("p (t h m) -> p h t m", t=PACK, m=LINE),
            in_=wx_words_raw[:].rearrange("p (h m t) -> p h t m", t=PACK, m=LINE),
        )
        nc.vector.tensor_copy(
            out=wx_q[1][:].rearrange("p (t m) -> p t m", t=PACK),
            in_=wx_scales_raw[:].rearrange("p (m t) -> p t m", t=PACK),
        )

        sums = {}
        for u, width in enumerate(UNITS):
            per_bank = BANK // width
            q, lo = divmod(STARTS[u], QUARTER)
            for t in range(PACK):
                if t % per_bank == 0:
                    bank = STARTS[u] // P + t // per_bank
                    group = psum.tile([P, per_bank, width], F32, name="sum%d" % bank, tag="bank%d" % bank)
                sums[u, t] = group[:, t % per_bank, :]
                mx_pass(sums[u, t], wx_q, t, c_q[q], span(lo, width), t % per_bank == 0, False)
                mx_pass(sums[u, t], wx_q, t, c_r[q], span(lo, width), False, False)

        picked_all = keep.tile([P, PACK * J], F32, name="picked_all", tag="c_then_picked")

        def picked(cols):
            h = cols.start // HALF
            half = picked_all[:, span(h * PACK * HALF, PACK * HALF)].rearrange("p (t j) -> p t j", t=PACK)
            return half[:, :, cols.start - h * HALF : cols.stop - h * HALF]

        def gather(t, cols):
            lists = offsets[:, cols.start // GROUP : cols.stop // GROUP]
            nc.vector.tensor_tensor(picked(cols)[:, t, :], x_planes[t][:].indirect(lists), wgt_sb[:, cols], ALU.mult)

        def gather_plane(t):
            gather(t, slice(0, HALF))
            gather(t, slice(HALF, J))

        gather_plane(0)
        gather_plane(1)

        wt_q = operand("wt", N)
        wt_woven = keep.tile([P, PACK * N], BF16, name="wt_woven", tag="x_plane0", align_bytes=64)
        nc.scalar.copy(
            out=wt_woven[:].rearrange("p (t m i) -> p m i t", t=PACK, i=PACK),
            in_=wt_raw[:].rearrange("p i (m t) -> p m i t", t=PACK),
        )
        quantize(wt_q, slice(0, N), wt_woven[:])

        gather_plane(2)

        x_woven = [
            keep.tile([P, PACK * width], BF16, name="x_woven%d" % u, align_bytes=64) for u, width in enumerate(UNITS)
        ]
        xg_q = [operand("xg%d" % u, width) for u, width in enumerate(UNITS)]
        y_quarters = [keep.tile([P, PACK, QUARTER], F32, name="y%d" % q) for q in range(J // QUARTER)]
        y_woven = [
            keep.tile([P, PACK * width], BF16, name="y_woven%d" % u, align_bytes=64) for u, width in enumerate(UNITS)
        ]
        y_q = operand("y", J)

        def unit_cols(u):
            return span(STARTS[u], UNITS[u])

        def y_planes(u):
            q, lo = divmod(STARTS[u], QUARTER)
            return y_quarters[q][:, :, span(lo, UNITS[u])]

        def weave_x(u):
            weave(u in WOVEN_ON_VECTOR, x_woven[u][:], picked(unit_cols(u)))

        def close_sums(u):
            per_bank = BANK // UNITS[u]
            quantize(xg_q[u], slice(0, UNITS[u]), x_woven[u][:])
            for t in range(PACK):
                mx_pass(sums[u, t], wt_q, t, xg_q[u], slice(0, UNITS[u]), False, t % per_bank == per_bank - 1)

        def finish(u):
            for t in range(PACK):
                nc.scalar.activation(out=y_planes(u)[:, t, :], in_=sums[u, t], func=ACT.Silu, bias=bias[:, t : t + 1])
            rows = out_0.rearrange("(p t) j -> p t j", t=PACK)
            nc.sync.dma_start(out=rows[:, :, unit_cols(u)], in_=y_planes(u))

        def store_words(cols):
            words = out_1[0].rearrange("p j i -> p (j i)").bitcast(I32)
            nc.sync.dma_start(out=words[:, cols], in_=y_q[0][:, cols].bitcast(I32))

        lead = HALF // UNITS[0]
        for u in range(lead):
            gather(PACK - 1, unit_cols(u))
            weave_x(u)
        gather(PACK - 1, slice(HALF, J))
        for u in range(len(UNITS) + 1):
            if u < len(UNITS):
                close_sums(u)
            if u + lead < len(UNITS):
                weave_x(u + lead)
            if u > 0:
                finish(u - 1)

        for u in range(len(UNITS) + 1):
            if u < len(UNITS):
                weave(True, y_woven[u][:], y_planes(u))
            if u > 0:
                quantize(y_q, unit_cols(u - 1), y_woven[u - 1][:])
            if u == WIDE_UNITS:
                store_words(slice(0, STARTS[WIDE_UNITS]))
        store_words(slice(STARTS[WIDE_UNITS], J))
        for quadrant in range(QUADRANTS):
            queue = nc.scalar if quadrant % 2 else nc.sync
            queue.dma_start(
                out=out_2[0, span(4 * quadrant, 4), :].bitcast(I32),
                in_=y_q[1][span(32 * quadrant, 4), :].bitcast(I32),
            )
